import numpy as np
import ml_dtypes


def mxq(x, axis, fmt="e4m3"):
    dtype, down = {"e4m3": (ml_dtypes.float8_e4m3fn, 7), "e5m2": (ml_dtypes.float8_e5m2, 14)}[fmt]
    v = np.moveaxis(np.asarray(x, np.float32).astype(ml_dtypes.bfloat16).astype(np.float64), axis, -1)
    blocks = v.reshape(v.shape[:-1] + (-1, 32))
    amax = np.abs(blocks).max(-1, keepdims=True)
    byte = np.maximum(np.where(amax > 0, np.frexp(amax)[1] - 1 + 127, 0) - down, 1)
    scale = np.exp2(byte - 127.0)
    codes = (blocks / scale).astype(np.float32).astype(dtype).astype(np.float64)
    return np.moveaxis((codes * scale).reshape(v.shape), -1, axis)


WIDE = False


def mx_kscale(k):
    if not WIDE:
        return np.ones(k)
    levels = np.array([10, -10, 5, -5, 0])
    if k % 512:
        return np.exp2(np.random.permutation(np.resize(levels, k // 32))).repeat(32)
    a = np.empty((k // 512, 16))
    for p in range(k // 512):
        a[p, :8] = np.random.permutation(np.resize(levels, 8))
        for g in range(8):
            far = levels[np.abs(levels - a[p, g]) >= 10]
            a[p, g + 8] = far[np.random.randint(len(far))]
    return np.exp2(a.ravel()).repeat(32)


def f64(x):
    return np.asarray(x).astype(np.float64)


def striped(idx):
    return np.tile(idx.reshape(-1, 16).T, (8, 1)).astype(np.uint16)


def unstriped(offs):
    return offs[:16].T.reshape(-1).astype(np.int64)


def relu(v):
    return np.maximum(v, 0.0)


K, T, E, C, N = 512, 2048, 8, 256, 512


def by_expert(wq, xq):
    return np.concatenate([wq[e].T @ xq[:, e * C:(e + 1) * C] for e in range(E)], axis=1)


def setup_inputs():
    n = np.random.standard_normal
    s = mx_kscale(K)[:, None]
    return {
        "xT": (n((K, T)) * s).astype(np.float32),
        "w": (n((E, K, N)) / np.sqrt(K) / s[None]).astype(np.float32),
        "b": (0.3 * n((N, E))).astype(np.float32),
        "gate": np.tile(np.random.uniform(0.2, 1.0, E * C), (N, 1)).astype(np.float32),
        "offs": striped(np.random.permutation(T)[:E * C]),
    }


def reference(xT, w, b, gate, offs):
    idx = unstriped(offs)
    xq = mxq(f64(xT)[:, idx], 0, "e4m3")
    y = by_expert(mxq(f64(w), 1, "e4m3"), xq)
    y = relu(y + np.repeat(f64(b), C, axis=1))
    out = np.zeros((N, T))
    out[:, idx] = f64(gate) * y
    return out

@@ -1,0 +1,155 @@
+from contextlib import ExitStack
+
+import concourse.mybir as mybir
+
+K, T, E, C, N = 512, 2048, 8, 256, 512
+
+F32 = mybir.dt.float32
+BF16 = mybir.dt.bfloat16
+U32 = mybir.dt.uint32
+U16 = mybir.dt.uint16
+U8 = mybir.dt.uint8
+FP8X4 = mybir.dt.float8_e4m3fn_x4
+MULT = mybir.AluOpType.mult
+ADD = mybir.AluOpType.add
+RELU = mybir.ActivationFunctionType.Relu
+
+P = 128
+PACK = 4
+BLOCKS = N // P
+GROUP = 2
+GROUPS = E // GROUP
+SLOTS = GROUP * C
+LIST_COLS = SLOTS // 16
+CHUNK = 1024
+SPLIT = 320
+
+FLOPS = 2 * K * N * E * C
+BYTES = 4 * (K * T + E * K * N + N * E + T + N * T) + 2 * 16 * (T // 16)
+
+
+def tile_routed_moe_kernel(tc, xT, w, b, gate, offs, out):
+    nc = tc.nc
+    with ExitStack() as ctx:
+        keep = ctx.enter_context(tc.tile_pool(name="keep", bufs=1))
+        load = ctx.enter_context(tc.tile_pool(name="load", bufs=10))
+        stage = ctx.enter_context(tc.tile_pool(name="stage", bufs=3))
+        work = ctx.enter_context(tc.tile_pool(name="work", bufs=12))
+        psum = ctx.enter_context(tc.psum_pool(name="psum", bufs=8))
+
+        offsets = keep.tile([P, T // 16], U16, name="offsets")
+        nc.sync.dma_start(offsets[:], offs)
+        x_rows = xT.rearrange("(p u j) t -> u p j t", u=2, j=2)
+        x_raw = {}
+        for u in range(2):
+            for c in range(T // CHUNK):
+                raw = load.tile([P, 2, CHUNK], F32, name="raw")
+                nc.sync.dma_start(raw[:], x_rows[u, :, :, c * CHUNK : (c + 1) * CHUNK])
+                x_raw[u, c] = raw
+        bias = keep.tile([P, BLOCKS, E], F32, name="bias")
+        nc.sync.dma_start(bias[:], b.rearrange("(n p) e -> p n e", p=P))
+        w_raw = []
+        for e in range(E):
+            raw = load.tile([P, PACK, N], F32, name="raw")
+            nc.sync.dma_start(raw[:], w[e].rearrange("(p j) n -> p j n", j=PACK))
+            w_raw.append(raw)
+            if e == 0:
+                gates = keep.tile([P, T], F32, name="gates")
+                nc.sync.dma_start(gates[:], gate[0:P, :])
+
+        warm = keep.tile([P, 1], F32, name="warm")
+        nc.vector.memset(warm[:], 0.0)
+        nc.scalar.activation(warm[:], warm[:], RELU)
+
+        pairs = []
+        for u in range(2):
+            pair = keep.tile([P, T, 2], BF16, name=f"pair{u}")
+            for c in range(T // CHUNK):
+                for h in range(2):
+                    lo = h * (CHUNK // 2)
+                    hi = lo + CHUNK // 2
+                    dst = pair[:, c * CHUNK + lo : c * CHUNK + hi, :]
+                    src = x_raw[u, c][:, :, lo:hi].rearrange("p j t -> p t j")
+                    if u == 0 and h == 0:
+                        nc.vector.tensor_copy(dst, src)
+                    else:
+                        nc.scalar.copy(dst, src)
+            pairs.append(pair)
+        windows = [pair[:].rearrange("p t j -> p (t j)").bitcast(U32) for pair in pairs]
+
+        grouped = [keep.tile([P, SLOTS, PACK], BF16, name=f"grouped{g}", align_bytes=64) for g in range(GROUPS)]
+
+        def gather(u, g):
+            words = grouped[g][:].rearrange("p s j -> p (s j)").bitcast(U32).rearrange("p (s u) -> p s u", u=2)
+            nc.vector.tensor_copy(words[:, :, u], windows[u].indirect(offsets[:, g * LIST_COLS : (g + 1) * LIST_COLS]))
+
+        x_codes = [keep.tile([P, SLOTS], U32, name=f"x_codes{g}", align_bytes=64) for g in range(GROUPS)]
+        x_scales = [keep.tile([P, SLOTS], U8, name=f"x_scales{g}", align_bytes=64) for g in range(GROUPS)]
+        results = [keep.tile([P, T], F32, name=f"result{n}") for n in range(BLOCKS)]
+
+        for g in range(GROUPS):
+            gather(0, g)
+        gather(1, 0)
+        for g in range(GROUPS):
+            if g + 1 < GROUPS:
+                gather(1, g + 1)
+            nc.vector.quantize_mx(
+                out=x_codes[g][:].bitcast(FP8X4),
+                scales=x_scales[g][:],
+                in_=grouped[g][:].rearrange("p s j -> p (s j)"),
+            )
+
+        w_codes = [keep.tile([P, N], U32, name=f"w_codes{e}", align_bytes=64) for e in range(E)]
+        w_scales = [keep.tile([P, N], U8, name=f"w_scales{e}", align_bytes=64) for e in range(E)]
+
+        def quantise_weights(g):
+            for e in range(g * GROUP, (g + 1) * GROUP):
+                w_grouped = stage.tile([P, N, PACK], BF16, name="w_grouped", align_bytes=64)
+                src = w_raw[e][:].rearrange("p j n -> p n j")
+                nc.scalar.copy(w_grouped[:, :SPLIT, :], src[:, :SPLIT, :])
+                nc.gpsimd.tensor_scalar(w_grouped[:, SPLIT:, :], src[:, SPLIT:, :], 1.0, 0.0, MULT, ADD)
+                nc.vector.quantize_mx(
+                    out=w_codes[e][:].bitcast(FP8X4),
+                    scales=w_scales[e][:],
+                    in_=w_grouped[:].rearrange("p n j -> p (n j)"),
+                )
+
+        def multiply(g):
+            ys = [work.tile([P, SLOTS], F32, name="y") for n in range(BLOCKS)]
+            for i in range(GROUP):
+                e = g * GROUP + i
+                slots = slice(i * C, (i + 1) * C)
+                for n in range(BLOCKS):
+                    cols = slice(n * P, (n + 1) * P)
+                    acc = psum.tile([P, C], F32, name="acc")
+                    nc.tensor.matmul_mx(
+                        out=acc[:],
+                        lhsT=w_codes[e][:, cols].bitcast(FP8X4),
+                        lhsT_scale=w_scales[e][:, cols],
+                        rhs=x_codes[g][:, slots].bitcast(FP8X4),
+                        rhs_scale=x_scales[g][:, slots],
+                        start=True,
+                        stop=True,
+                    )
+                    nc.scalar.activation(ys[n][:, slots], acc[:], RELU, bias=bias[:, n, e : e + 1])
+            for n in range(BLOCKS):
+                nc.gpsimd.tensor_tensor(ys[n][:], ys[n][:], gates[:, g * SLOTS : (g + 1) * SLOTS], MULT)
+            return ys
+
+        def put_back(g, ys):
+            for n in range(BLOCKS):
+                nc.vector.tensor_copy(results[n][:].indirect(offsets[:, g * LIST_COLS : (g + 1) * LIST_COLS]), ys[n][:])
+
+        quantise_weights(0)
+        quantise_weights(1)
+        ys = multiply(0)
+        for g in range(GROUPS):
+            if g + 2 < GROUPS:
+                quantise_weights(g + 2)
+            if g + 1 < GROUPS:
+                ahead = multiply(g + 1)
+            put_back(g, ys)
+            ys = ahead
+
+        for n in range(BLOCKS):
+            nc.sync.dma_start(out[n * P : (n + 1) * P, :], results[n][:])

@@ -11,18 +11,16 @@ U16 = mybir.dt.uint16
 U8 = mybir.dt.uint8
 FP8X4 = mybir.dt.float8_e4m3fn_x4
 MULT = mybir.AluOpType.mult
-ADD = mybir.AluOpType.add
 RELU = mybir.ActivationFunctionType.Relu
+COPY = mybir.ActivationFunctionType.Copy
 
 P = 128
 PACK = 4
 BLOCKS = N // P
-GROUP = 2
-GROUPS = E // GROUP
-SLOTS = GROUP * C
-LIST_COLS = SLOTS // 16
-CHUNK = 1024
-SPLIT = 320
+LIST_COLS = C // 16
+PAIR_CHUNK = 512
+PLANE_CHUNK = 1024
+HALF = N // 2
 
 FLOPS = 2 * K * N * E * C
 BYTES = 4 * (K * T + E * K * N + N * E + T + N * T) + 2 * 16 * (T // 16)
@@ -32,124 +30,146 @@ def tile_routed_moe_kernel(tc, xT, w, b, gate, offs, out):
     nc = tc.nc
     with ExitStack() as ctx:
         keep = ctx.enter_context(tc.tile_pool(name="keep", bufs=1))
-        load = ctx.enter_context(tc.tile_pool(name="load", bufs=10))
         stage = ctx.enter_context(tc.tile_pool(name="stage", bufs=3))
-        work = ctx.enter_context(tc.tile_pool(name="work", bufs=12))
+        work = ctx.enter_context(tc.tile_pool(name="work", bufs=16))
         psum = ctx.enter_context(tc.psum_pool(name="psum", bufs=8))
 
         offsets = keep.tile([P, T // 16], U16, name="offsets")
         nc.sync.dma_start(offsets[:], offs)
-        x_rows = xT.rearrange("(p u j) t -> u p j t", u=2, j=2)
-        x_raw = {}
-        for u in range(2):
-            for c in range(T // CHUNK):
-                raw = load.tile([P, 2, CHUNK], F32, name="raw")
-                nc.sync.dma_start(raw[:], x_rows[u, :, :, c * CHUNK : (c + 1) * CHUNK])
-                x_raw[u, c] = raw
+        x_rows = xT.rearrange("(p t) n -> p t n", t=PACK)
+        pair_raw = []
+        for c in range(T // PAIR_CHUNK):
+            raw = keep.tile([P, 2, PAIR_CHUNK], F32, name=f"pair_raw{c}")
+            nc.sync.dma_start(raw[:], x_rows[:, 0:2, c * PAIR_CHUNK : (c + 1) * PAIR_CHUNK])
+            pair_raw.append(raw)
+        plane_raw = {}
+        for t in (2, 3):
+            for c in range(T // PLANE_CHUNK):
+                raw = keep.tile([P, PLANE_CHUNK], F32, name=f"plane_raw{t}_{c}")
+                nc.sync.dma_start(raw[:], x_rows[:, t, c * PLANE_CHUNK : (c + 1) * PLANE_CHUNK])
+                plane_raw[t, c] = raw
         bias = keep.tile([P, BLOCKS, E], F32, name="bias")
         nc.sync.dma_start(bias[:], b.rearrange("(n p) e -> p n e", p=P))
-        w_raw = []
+        gates = [keep.tile([P, 2 * C], F32, name="gates0"), keep.tile([P, T - 2 * C], F32, name="gates1")]
+        w_raw = {}
         for e in range(E):
-            raw = load.tile([P, PACK, N], F32, name="raw")
-            nc.sync.dma_start(raw[:], w[e].rearrange("(p j) n -> p j n", j=PACK))
-            w_raw.append(raw)
+            rows = w[e].rearrange("(p j) n -> p j n", j=PACK)
             if e == 0:
-                gates = keep.tile([P, T], F32, name="gates")
-                nc.sync.dma_start(gates[:], gate[0:P, :])
+                for h in range(2):
+                    raw = keep.tile([P, PACK, HALF], F32, name=f"w_raw0_{h}")
+                    nc.sync.dma_start(raw[:], rows[:, :, h * HALF : (h + 1) * HALF])
+                    w_raw[e, h] = raw[:]
+                    if h == 0:
+                        nc.sync.dma_start(gates[0][:], gate[0:P, 0 : 2 * C])
+            else:
+                raw = keep.tile([P, PACK, N], F32, name=f"w_raw{e}")
+                nc.sync.dma_start(raw[:], rows)
+                for h in range(2):
+                    w_raw[e, h] = raw[:, :, h * HALF : (h + 1) * HALF]
+            if e == 1:
+                nc.sync.dma_start(gates[1][:], gate[0:P, 2 * C : T])
+
+        def gate_of(e):
+            return gates[0][:, e * C : (e + 1) * C] if e < 2 else gates[1][:, (e - 2) * C : (e - 1) * C]
+
+        def list_of(e):
+            return offsets[:, e * LIST_COLS : (e + 1) * LIST_COLS]
 
         warm = keep.tile([P, 1], F32, name="warm")
         nc.vector.memset(warm[:], 0.0)
         nc.scalar.activation(warm[:], warm[:], RELU)
 
-        pairs = []
-        for u in range(2):
-            pair = keep.tile([P, T, 2], BF16, name=f"pair{u}")
-            for c in range(T // CHUNK):
-                for h in range(2):
-                    lo = h * (CHUNK // 2)
-                    hi = lo + CHUNK // 2
-                    dst = pair[:, c * CHUNK + lo : c * CHUNK + hi, :]
-                    src = x_raw[u, c][:, :, lo:hi].rearrange("p j t -> p t j")
-                    if u == 0 and h == 0:
-                        nc.vector.tensor_copy(dst, src)
-                    else:
-                        nc.scalar.copy(dst, src)
-            pairs.append(pair)
-        windows = [pair[:].rearrange("p t j -> p (t j)").bitcast(U32) for pair in pairs]
-
-        grouped = [keep.tile([P, SLOTS, PACK], BF16, name=f"grouped{g}", align_bytes=64) for g in range(GROUPS)]
-
-        def gather(u, g):
-            words = grouped[g][:].rearrange("p s j -> p (s j)").bitcast(U32).rearrange("p (s u) -> p s u", u=2)
-            nc.vector.tensor_copy(words[:, :, u], windows[u].indirect(offsets[:, g * LIST_COLS : (g + 1) * LIST_COLS]))
-
-        x_codes = [keep.tile([P, SLOTS], U32, name=f"x_codes{g}", align_bytes=64) for g in range(GROUPS)]
-        x_scales = [keep.tile([P, SLOTS], U8, name=f"x_scales{g}", align_bytes=64) for g in range(GROUPS)]
-        results = [keep.tile([P, T], F32, name=f"result{n}") for n in range(BLOCKS)]
-
-        for g in range(GROUPS):
-            gather(0, g)
-        gather(1, 0)
-        for g in range(GROUPS):
-            if g + 1 < GROUPS:
-                gather(1, g + 1)
-            nc.vector.quantize_mx(
-                out=x_codes[g][:].bitcast(FP8X4),
-                scales=x_scales[g][:],
-                in_=grouped[g][:].rearrange("p s j -> p (s j)"),
+        pair = keep.tile([P, T, 2], BF16, name="pair")
+        for c in range(T // PAIR_CHUNK):
+            nc.vector.tensor_copy(
+                pair[:, c * PAIR_CHUNK : (c + 1) * PAIR_CHUNK, :], pair_raw[c][:].rearrange("p j t -> p t j")
             )
+        words = pair[:].rearrange("p t j -> p (t j)").bitcast(U32)
+        planes = {t: keep.tile([P, T], BF16, name=f"plane{t}") for t in (2, 3)}
 
+        grouped = [keep.tile([P, C, PACK], BF16, name=f"grouped{e}", align_bytes=64) for e in range(E)]
+        x_codes = [keep.tile([P, C], U32, name=f"x_codes{e}", align_bytes=64) for e in range(E)]
+        x_scales = [keep.tile([P, C], U8, name=f"x_scales{e}", align_bytes=64) for e in range(E)]
         w_codes = [keep.tile([P, N], U32, name=f"w_codes{e}", align_bytes=64) for e in range(E)]
         w_scales = [keep.tile([P, N], U8, name=f"w_scales{e}", align_bytes=64) for e in range(E)]
+        results = [keep.tile([P, T], F32, name=f"result{n}") for n in range(BLOCKS)]
 
-        def quantise_weights(g):
-            for e in range(g * GROUP, (g + 1) * GROUP):
-                w_grouped = stage.tile([P, N, PACK], BF16, name="w_grouped", align_bytes=64)
-                src = w_raw[e][:].rearrange("p j n -> p n j")
-                nc.scalar.copy(w_grouped[:, :SPLIT, :], src[:, :SPLIT, :])
-                nc.gpsimd.tensor_scalar(w_grouped[:, SPLIT:, :], src[:, SPLIT:, :], 1.0, 0.0, MULT, ADD)
+        def gather_pair(e):
+            dst = grouped[e][:].rearrange("p s j -> p (s j)").bitcast(U32).rearrange("p (s u) -> p s u", u=2)
+            nc.vector.tensor_copy(dst[:, :, 0], words.indirect(list_of(e)))
+
+        def gather_plane(e, t):
+            nc.scalar.activation(grouped[e][:, :, t], planes[t][:].indirect(list_of(e)), COPY)
+
+        def quantise_tokens(e):
+            nc.vector.quantize_mx(
+                out=x_codes[e][:].bitcast(FP8X4),
+                scales=x_scales[e][:],
+                in_=grouped[e][:].rearrange("p s j -> p (s j)"),
+            )
+
+        def quantise_weights(e, copy):
+            for h in range(2):
+                w_grouped = stage.tile([P, HALF, PACK], BF16, name="w_grouped", align_bytes=64)
+                copy(w_grouped[:], w_raw[e, h].rearrange("p j n -> p n j"))
+                cols = slice(h * HALF, (h + 1) * HALF)
                 nc.vector.quantize_mx(
-                    out=w_codes[e][:].bitcast(FP8X4),
-                    scales=w_scales[e][:],
+                    out=w_codes[e][:, cols].bitcast(FP8X4),
+                    scales=w_scales[e][:, cols],
                     in_=w_grouped[:].rearrange("p n j -> p (n j)"),
                 )
 
-        def multiply(g):
-            ys = [work.tile([P, SLOTS], F32, name="y") for n in range(BLOCKS)]
-            for i in range(GROUP):
-                e = g * GROUP + i
-                slots = slice(i * C, (i + 1) * C)
-                for n in range(BLOCKS):
-                    cols = slice(n * P, (n + 1) * P)
-                    acc = psum.tile([P, C], F32, name="acc")
-                    nc.tensor.matmul_mx(
-                        out=acc[:],
-                        lhsT=w_codes[e][:, cols].bitcast(FP8X4),
-                        lhsT_scale=w_scales[e][:, cols],
-                        rhs=x_codes[g][:, slots].bitcast(FP8X4),
-                        rhs_scale=x_scales[g][:, slots],
-                        start=True,
-                        stop=True,
-                    )
-                    nc.scalar.activation(ys[n][:, slots], acc[:], RELU, bias=bias[:, n, e : e + 1])
+        def multiply(e):
+            ys = []
             for n in range(BLOCKS):
-                nc.gpsimd.tensor_tensor(ys[n][:], ys[n][:], gates[:, g * SLOTS : (g + 1) * SLOTS], MULT)
+                cols = slice(n * P, (n + 1) * P)
+                acc = psum.tile([P, C], F32, name="acc")
+                nc.tensor.matmul_mx(
+                    out=acc[:],
+                    lhsT=w_codes[e][:, cols].bitcast(FP8X4),
+                    lhsT_scale=w_scales[e][:, cols],
+                    rhs=x_codes[e][:].bitcast(FP8X4),
+                    rhs_scale=x_scales[e][:],
+                    start=True,
+                    stop=True,
+                )
+                y = work.tile([P, C], F32, name="y")
+                nc.scalar.activation(y[:], acc[:], RELU, bias=bias[:, n, e : e + 1])
+                ys.append(y)
             return ys
 
-        def put_back(g, ys):
-            for n in range(BLOCKS):
-                nc.vector.tensor_copy(results[n][:].indirect(offsets[:, g * LIST_COLS : (g + 1) * LIST_COLS]), ys[n][:])
+        def put_back(e, n, y):
+            nc.vector.tensor_tensor(results[n][:].indirect(list_of(e)), y[:], gate_of(e), MULT)
 
-        quantise_weights(0)
-        quantise_weights(1)
-        ys = multiply(0)
-        for g in range(GROUPS):
-            if g + 2 < GROUPS:
-                quantise_weights(g + 2)
-            if g + 1 < GROUPS:
-                ahead = multiply(g + 1)
-            put_back(g, ys)
-            ys = ahead
+        def prepare(e):
+            gather_pair(e)
+            for t in (2, 3):
+                gather_plane(e, t)
+            quantise_tokens(e)
+            quantise_weights(e, nc.scalar.copy)
+
+        gather_pair(0)
+        for t in (2, 3):
+            for c in range(T // PLANE_CHUNK):
+                dst = planes[t][:, c * PLANE_CHUNK : (c + 1) * PLANE_CHUNK]
+                if (t, c) == (3, 1):
+                    nc.vector.tensor_copy(dst, plane_raw[t, c][:])
+                else:
+                    nc.scalar.copy(dst, plane_raw[t, c][:])
+            gather_plane(0, t)
+        quantise_tokens(0)
+        quantise_weights(0, nc.vector.tensor_copy)
+        ys = [multiply(0)]
+        prepare(1)
+        prepare(2)
+        ys.append(multiply(1))
+        for e in range(E):
+            for n in range(BLOCKS):
+                put_back(e, n, ys[e][n])
+            if e + 3 < E:
+                prepare(e + 3)
+            if e + 2 < E:
+                ys.append(multiply(e + 2))
 
         for n in range(BLOCKS):
             nc.sync.dma_start(out[n * P : (n + 1) * P, :], results[n][:])

@@ -17,8 +17,11 @@ COPY = mybir.ActivationFunctionType.Copy
 P = 128
 PACK = 4
 BLOCKS = N // P
-LIST_COLS = C // 16
-PAIR_CHUNK = 512
+SCATTERS = [[0], [1], [2], [3], [4], [5], [6, 7]]
+BY_PAIRS = 4
+GATHER_AHEAD = [1, 1, 2, 2, 2, 2, 2, 2]
+WEIGHTS_AHEAD = [1, 1, 1, 1, 1, 2, 2, 2]
+PAIR_CHUNKS = [(0, 1024), (1024, 1536), (1536, 2048)]
 PLANE_CHUNK = 1024
 HALF = N // 2
 
@@ -30,76 +33,94 @@ def tile_routed_moe_kernel(tc, xT, w, b, gate, offs, out):
     nc = tc.nc
     with ExitStack() as ctx:
         keep = ctx.enter_context(tc.tile_pool(name="keep", bufs=1))
-        stage = ctx.enter_context(tc.tile_pool(name="stage", bufs=3))
-        work = ctx.enter_context(tc.tile_pool(name="work", bufs=16))
+        stage = ctx.enter_context(tc.tile_pool(name="stage", bufs=2))
+        work = ctx.enter_context(tc.tile_pool(name="work", bufs=12))
+        ring = ctx.enter_context(tc.tile_pool(name="ring", bufs=2))
         psum = ctx.enter_context(tc.psum_pool(name="psum", bufs=8))
 
         offsets = keep.tile([P, T // 16], U16, name="offsets")
         nc.sync.dma_start(offsets[:], offs)
         x_rows = xT.rearrange("(p t) n -> p t n", t=PACK)
         pair_raw = []
-        for c in range(T // PAIR_CHUNK):
-            raw = keep.tile([P, 2, PAIR_CHUNK], F32, name=f"pair_raw{c}")
-            nc.sync.dma_start(raw[:], x_rows[:, 0:2, c * PAIR_CHUNK : (c + 1) * PAIR_CHUNK])
+        for lo, hi in PAIR_CHUNKS:
+            raw = keep.tile([P, 2, hi - lo], F32, name=f"pair_raw{lo}")
+            nc.sync.dma_start(raw[:], x_rows[:, 0:2, lo:hi])
             pair_raw.append(raw)
         plane_raw = {}
-        for t in (2, 3):
+
+        def load_plane(t):
             for c in range(T // PLANE_CHUNK):
                 raw = keep.tile([P, PLANE_CHUNK], F32, name=f"plane_raw{t}_{c}")
                 nc.sync.dma_start(raw[:], x_rows[:, t, c * PLANE_CHUNK : (c + 1) * PLANE_CHUNK])
                 plane_raw[t, c] = raw
-        bias = keep.tile([P, BLOCKS, E], F32, name="bias")
-        nc.sync.dma_start(bias[:], b.rearrange("(n p) e -> p n e", p=P))
-        gates = [keep.tile([P, 2 * C], F32, name="gates0"), keep.tile([P, T - 2 * C], F32, name="gates1")]
+
         w_raw = {}
-        for e in range(E):
-            rows = w[e].rearrange("(p j) n -> p j n", j=PACK)
-            if e == 0:
-                for h in range(2):
-                    raw = keep.tile([P, PACK, HALF], F32, name=f"w_raw0_{h}")
-                    nc.sync.dma_start(raw[:], rows[:, :, h * HALF : (h + 1) * HALF])
-                    w_raw[e, h] = raw[:]
-                    if h == 0:
-                        nc.sync.dma_start(gates[0][:], gate[0:P, 0 : 2 * C])
-            else:
-                raw = keep.tile([P, PACK, N], F32, name=f"w_raw{e}")
-                nc.sync.dma_start(raw[:], rows)
-                for h in range(2):
-                    w_raw[e, h] = raw[:, :, h * HALF : (h + 1) * HALF]
-            if e == 1:
-                nc.sync.dma_start(gates[1][:], gate[0:P, 2 * C : T])
 
-        def gate_of(e):
-            return gates[0][:, e * C : (e + 1) * C] if e < 2 else gates[1][:, (e - 2) * C : (e - 1) * C]
+        def load_weights(e):
+            raw = keep.tile([P, PACK, N], F32, name=f"w_raw{e}")
+            nc.sync.dma_start(raw[:], w[e].rearrange("(p j) n -> p j n", j=PACK))
+            w_raw[e, 0] = raw
 
-        def list_of(e):
-            return offsets[:, e * LIST_COLS : (e + 1) * LIST_COLS]
+        load_plane(2)
+        bias = keep.tile([P, BLOCKS, E], F32, name="bias")
+        first_gates = keep.tile([P, C], F32, name="first_gates")
+        rest_gates = keep.tile([P, T - C], F32, name="rest_gates")
+        load_plane(3)
+        rows = w[0].rearrange("(p j) n -> p j n", j=PACK)
+        for h in range(2):
+            raw = keep.tile([P, PACK, HALF], F32, name=f"w_raw0_{h}")
+            nc.sync.dma_start(raw[:], rows[:, :, h * HALF : (h + 1) * HALF])
+            w_raw[0, h] = raw
+            if h == 0:
+                nc.sync.dma_start(first_gates[:], gate[0:P, 0:C])
+        nc.sync.dma_start(bias[:], b.rearrange("(n p) e -> p n e", p=P))
+        load_weights(1)
+        nc.sync.dma_start(rest_gates[:], gate[0:P, C:T])
+        for e in range(2, E):
+            load_weights(e)
+
+        def gate_of(experts):
+            lo, hi = experts[0] * C, (experts[-1] + 1) * C
+            return first_gates[:] if lo == 0 else rest_gates[:, lo - C : hi - C]
+
+        def list_of(experts):
+            return offsets[:, experts[0] * C // 16 : (experts[-1] + 1) * C // 16]
 
         warm = keep.tile([P, 1], F32, name="warm")
         nc.vector.memset(warm[:], 0.0)
         nc.scalar.activation(warm[:], warm[:], RELU)
 
         pair = keep.tile([P, T, 2], BF16, name="pair")
-        for c in range(T // PAIR_CHUNK):
-            nc.vector.tensor_copy(
-                pair[:, c * PAIR_CHUNK : (c + 1) * PAIR_CHUNK, :], pair_raw[c][:].rearrange("p j t -> p t j")
-            )
+        for (lo, hi), raw in zip(PAIR_CHUNKS, pair_raw):
+            copy = nc.scalar.copy if lo == 0 else nc.vector.tensor_copy
+            copy(pair[:, lo:hi, :], raw[:].rearrange("p j t -> p t j"))
         words = pair[:].rearrange("p t j -> p (t j)").bitcast(U32)
-        planes = {t: keep.tile([P, T], BF16, name=f"plane{t}") for t in (2, 3)}
+        planes = {t: keep.tile([P, T], BF16, name=f"plane{t}") for t in range(PACK)}
 
-        grouped = [keep.tile([P, C, PACK], BF16, name=f"grouped{e}", align_bytes=64) for e in range(E)]
+        grouped = {}
         x_codes = [keep.tile([P, C], U32, name=f"x_codes{e}", align_bytes=64) for e in range(E)]
         x_scales = [keep.tile([P, C], U8, name=f"x_scales{e}", align_bytes=64) for e in range(E)]
         w_codes = [keep.tile([P, N], U32, name=f"w_codes{e}", align_bytes=64) for e in range(E)]
         w_scales = [keep.tile([P, N], U8, name=f"w_scales{e}", align_bytes=64) for e in range(E)]
         results = [keep.tile([P, T], F32, name=f"result{n}") for n in range(BLOCKS)]
 
+        def round_plane(t, c, copy):
+            copy(planes[t][:, c * PLANE_CHUNK : (c + 1) * PLANE_CHUNK], plane_raw[t, c][:])
+
+        def gather(e):
+            grouped[e] = ring.tile([P, C, PACK], BF16, name="grouped", align_bytes=64)
+            if e < BY_PAIRS:
+                gather_pair(e)
+            for t in range(2 if e < BY_PAIRS else 0, PACK):
+                gather_plane(e, t)
+            quantise_tokens(e)
+
         def gather_pair(e):
             dst = grouped[e][:].rearrange("p s j -> p (s j)").bitcast(U32).rearrange("p (s u) -> p s u", u=2)
-            nc.vector.tensor_copy(dst[:, :, 0], words.indirect(list_of(e)))
+            nc.vector.tensor_copy(dst[:, :, 0], words.indirect(list_of([e])))
 
         def gather_plane(e, t):
-            nc.scalar.activation(grouped[e][:, :, t], planes[t][:].indirect(list_of(e)), COPY)
+            nc.scalar.activation(grouped[e][:, :, t], planes[t][:].indirect(list_of([e])), COPY)
 
         def quantise_tokens(e):
             nc.vector.quantize_mx(
@@ -108,68 +129,74 @@ def tile_routed_moe_kernel(tc, xT, w, b, gate, offs, out):
                 in_=grouped[e][:].rearrange("p s j -> p (s j)"),
             )
 
-        def quantise_weights(e, copy):
-            for h in range(2):
-                w_grouped = stage.tile([P, HALF, PACK], BF16, name="w_grouped", align_bytes=64)
-                copy(w_grouped[:], w_raw[e, h].rearrange("p j n -> p n j"))
-                cols = slice(h * HALF, (h + 1) * HALF)
-                nc.vector.quantize_mx(
-                    out=w_codes[e][:, cols].bitcast(FP8X4),
-                    scales=w_scales[e][:, cols],
-                    in_=w_grouped[:].rearrange("p n j -> p (n j)"),
-                )
+        def quantise_weights(e, h, copy):
+            raw = w_raw[e, h]
+            width = raw.shape[2]
+            w_grouped = stage.tile([P, width, PACK], BF16, name="w_grouped", align_bytes=64)
+            copy(w_grouped[:], raw[:].rearrange("p j n -> p n j"))
+            cols = slice(h * width, (h + 1) * width)
+            nc.vector.quantize_mx(
+                out=w_codes[e][:, cols].bitcast(FP8X4),
+                scales=w_scales[e][:, cols],
+                in_=w_grouped[:].rearrange("p n j -> p (n j)"),
+            )
 
-        def multiply(e):
-            ys = []
+        group_of = {e: experts for experts in SCATTERS for e in experts}
+        ys = {}
+
+        def multiply(e, n):
+            experts = group_of[e]
+            cols = slice(n * P, (n + 1) * P)
+            acc = psum.tile([P, C], F32, name="acc")
+            nc.tensor.matmul_mx(
+                out=acc[:],
+                lhsT=w_codes[e][:, cols].bitcast(FP8X4),
+                lhsT_scale=w_scales[e][:, cols],
+                rhs=x_codes[e][:].bitcast(FP8X4),
+                rhs_scale=x_scales[e][:],
+                start=True,
+                stop=True,
+            )
+            if e == experts[0]:
+                y = work.tile([P, len(experts) * C], F32, name="y")
+                ys[e, n] = y
+            lo = (e - experts[0]) * C
+            nc.scalar.activation(ys[experts[0], n][:, lo : lo + C], acc[:], RELU, bias=bias[:, n, e : e + 1])
+
+        def put_back(experts):
             for n in range(BLOCKS):
-                cols = slice(n * P, (n + 1) * P)
-                acc = psum.tile([P, C], F32, name="acc")
-                nc.tensor.matmul_mx(
-                    out=acc[:],
-                    lhsT=w_codes[e][:, cols].bitcast(FP8X4),
-                    lhsT_scale=w_scales[e][:, cols],
-                    rhs=x_codes[e][:].bitcast(FP8X4),
-                    rhs_scale=x_scales[e][:],
-                    start=True,
-                    stop=True,
-                )
-                y = work.tile([P, C], F32, name="y")
-                nc.scalar.activation(y[:], acc[:], RELU, bias=bias[:, n, e : e + 1])
-                ys.append(y)
-            return ys
+                y = ys[experts[0], n]
+                nc.vector.tensor_tensor(results[n][:].indirect(list_of(experts)), y[:], gate_of(experts), MULT)
 
-        def put_back(e, n, y):
-            nc.vector.tensor_tensor(results[n][:].indirect(list_of(e)), y[:], gate_of(e), MULT)
-
-        def prepare(e):
-            gather_pair(e)
-            for t in (2, 3):
-                gather_plane(e, t)
-            quantise_tokens(e)
-            quantise_weights(e, nc.scalar.copy)
-
+        grouped[0] = ring.tile([P, C, PACK], BF16, name="grouped", align_bytes=64)
         gather_pair(0)
-        for t in (2, 3):
-            for c in range(T // PLANE_CHUNK):
-                dst = planes[t][:, c * PLANE_CHUNK : (c + 1) * PLANE_CHUNK]
-                if (t, c) == (3, 1):
-                    nc.vector.tensor_copy(dst, plane_raw[t, c][:])
-                else:
-                    nc.scalar.copy(dst, plane_raw[t, c][:])
-            gather_plane(0, t)
+        for t in (0, 1):
+            for (lo, hi), raw in zip(PAIR_CHUNKS, pair_raw):
+                nc.vector.tensor_copy(planes[t][:, lo:hi], raw[:, t, :])
+        round_plane(2, 0, nc.scalar.copy)
+        round_plane(2, 1, nc.vector.tensor_copy)
+        gather_plane(0, 2)
+        round_plane(3, 0, nc.vector.tensor_copy)
+        round_plane(3, 1, nc.vector.tensor_copy)
+        gather_plane(0, 3)
         quantise_tokens(0)
-        quantise_weights(0, nc.vector.tensor_copy)
-        ys = [multiply(0)]
-        prepare(1)
-        prepare(2)
-        ys.append(multiply(1))
+        for h in range(2):
+            quantise_weights(0, h, (nc.vector.tensor_copy, nc.scalar.copy)[h])
+            for n in (2 * h, 2 * h + 1):
+                multiply(0, n)
+        gathered, quantised = 0, 0
         for e in range(E):
-            for n in range(BLOCKS):
-                put_back(e, n, ys[e][n])
-            if e + 3 < E:
-                prepare(e + 3)
-            if e + 2 < E:
-                ys.append(multiply(e + 2))
+            while gathered < min(E - 1, e + GATHER_AHEAD[e]):
+                gathered += 1
+                gather(gathered)
+            while quantised < min(E - 1, e + WEIGHTS_AHEAD[e]):
+                quantised += 1
+                quantise_weights(quantised, 0, nc.scalar.copy)
+            if e > 0:
+                for n in range(BLOCKS):
+                    multiply(e, n)
+            if e == group_of[e][-1]:
+                put_back(group_of[e])
 
         for n in range(BLOCKS):
             nc.sync.dma_start(out[n * P : (n + 1) * P, :], results[n][:])

@@ -24,6 +24,7 @@ WEIGHTS_AHEAD = [1, 1, 1, 1, 1, 2, 2, 2]
 PAIR_CHUNKS = [(0, 1024), (1024, 1536), (1536, 2048)]
 PLANE_CHUNK = 1024
 HALF = N // 2
+RUN = 4
 
 FLOPS = 2 * K * N * E * C
 BYTES = 4 * (K * T + E * K * N + N * E + T + N * T) + 2 * 16 * (T // 16)
@@ -90,12 +91,18 @@ def tile_routed_moe_kernel(tc, xT, w, b, gate, offs, out):
         nc.vector.memset(warm[:], 0.0)
         nc.scalar.activation(warm[:], warm[:], RELU)
 
+        def interleave(copy, dst, src):
+            copy(
+                dst.rearrange("p (c i) j -> p c j i", i=RUN),
+                src.rearrange("p j (c i) -> p c j i", i=RUN),
+            )
+
         pair = keep.tile([P, T, 2], BF16, name="pair")
         for (lo, hi), raw in zip(PAIR_CHUNKS, pair_raw):
             copy = nc.scalar.copy if lo == 0 else nc.vector.tensor_copy
-            copy(pair[:, lo:hi, :], raw[:].rearrange("p j t -> p t j"))
+            interleave(copy, pair[:, lo:hi, :], raw[:])
         words = pair[:].rearrange("p t j -> p (t j)").bitcast(U32)
-        planes = {t: keep.tile([P, T], BF16, name=f"plane{t}") for t in range(PACK)}
+        planes = keep.tile([P, PACK, T], BF16, name="planes", align_bytes=64)
 
         grouped = {}
         x_codes = [keep.tile([P, C], U32, name=f"x_codes{e}", align_bytes=64) for e in range(E)]
@@ -105,7 +112,7 @@ def tile_routed_moe_kernel(tc, xT, w, b, gate, offs, out):
         results = [keep.tile([P, T], F32, name=f"result{n}") for n in range(BLOCKS)]
 
         def round_plane(t, c, copy):
-            copy(planes[t][:, c * PLANE_CHUNK : (c + 1) * PLANE_CHUNK], plane_raw[t, c][:])
+            copy(planes[:, t, c * PLANE_CHUNK : (c + 1) * PLANE_CHUNK], plane_raw[t, c][:])
 
         def gather(e):
             grouped[e] = ring.tile([P, C, PACK], BF16, name="grouped", align_bytes=64)
@@ -120,7 +127,7 @@ def tile_routed_moe_kernel(tc, xT, w, b, gate, offs, out):
             nc.vector.tensor_copy(dst[:, :, 0], words.indirect(list_of([e])))
 
         def gather_plane(e, t):
-            nc.scalar.activation(grouped[e][:, :, t], planes[t][:].indirect(list_of([e])), COPY)
+            nc.scalar.activation(grouped[e][:, :, t], planes[:, t, :].indirect(list_of([e])), COPY)
 
         def quantise_tokens(e):
             nc.vector.quantize_mx(
@@ -133,7 +140,7 @@ def tile_routed_moe_kernel(tc, xT, w, b, gate, offs, out):
             raw = w_raw[e, h]
             width = raw.shape[2]
             w_grouped = stage.tile([P, width, PACK], BF16, name="w_grouped", align_bytes=64)
-            copy(w_grouped[:], raw[:].rearrange("p j n -> p n j"))
+            interleave(copy, w_grouped[:], raw[:])
             cols = slice(h * width, (h + 1) * width)
             nc.vector.quantize_mx(
                 out=w_codes[e][:, cols].bitcast(FP8X4),
@@ -170,9 +177,8 @@ def tile_routed_moe_kernel(tc, xT, w, b, gate, offs, out):
 
         grouped[0] = ring.tile([P, C, PACK], BF16, name="grouped", align_bytes=64)
         gather_pair(0)
-        for t in (0, 1):
-            for (lo, hi), raw in zip(PAIR_CHUNKS, pair_raw):
-                nc.vector.tensor_copy(planes[t][:, lo:hi], raw[:, t, :])
+        for (lo, hi), raw in zip(PAIR_CHUNKS, pair_raw):
+            nc.vector.tensor_copy(planes[:, 0:2, lo:hi], raw[:])
         round_plane(2, 0, nc.scalar.copy)
         round_plane(2, 1, nc.vector.tensor_copy)
         gather_plane(0, 2)

from contextlib import ExitStack

import concourse.mybir as mybir

K, T, E, C, N = 512, 2048, 8, 256, 512

F32 = mybir.dt.float32
BF16 = mybir.dt.bfloat16
U32 = mybir.dt.uint32
U16 = mybir.dt.uint16
U8 = mybir.dt.uint8
FP8X4 = mybir.dt.float8_e4m3fn_x4
MULT = mybir.AluOpType.mult
RELU = mybir.ActivationFunctionType.Relu
COPY = mybir.ActivationFunctionType.Copy

P = 128
PACK = 4
BLOCKS = N // P
SCATTERS = [[0], [1], [2], [3], [4], [5], [6, 7]]
BY_PAIRS = 4
GATHER_AHEAD = [1, 1, 2, 2, 2, 2, 2, 2]
WEIGHTS_AHEAD = [1, 1, 1, 1, 1, 2, 2, 2]
PAIR_CHUNKS = [(0, 1024), (1024, 1536), (1536, 2048)]
PLANE_CHUNK = 1024
HALF = N // 2
RUN = 4

FLOPS = 2 * K * N * E * C
BYTES = 4 * (K * T + E * K * N + N * E + T + N * T) + 2 * 16 * (T // 16)


def tile_routed_moe_kernel(tc, xT, w, b, gate, offs, out):
    nc = tc.nc
    with ExitStack() as ctx:
        keep = ctx.enter_context(tc.tile_pool(name="keep", bufs=1))
        stage = ctx.enter_context(tc.tile_pool(name="stage", bufs=2))
        work = ctx.enter_context(tc.tile_pool(name="work", bufs=12))
        ring = ctx.enter_context(tc.tile_pool(name="ring", bufs=2))
        psum = ctx.enter_context(tc.psum_pool(name="psum", bufs=8))

        offsets = keep.tile([P, T // 16], U16, name="offsets")
        nc.sync.dma_start(offsets[:], offs)
        x_rows = xT.rearrange("(p t) n -> p t n", t=PACK)
        pair_raw = []
        for lo, hi in PAIR_CHUNKS:
            raw = keep.tile([P, 2, hi - lo], F32, name=f"pair_raw{lo}")
            nc.sync.dma_start(raw[:], x_rows[:, 0:2, lo:hi])
            pair_raw.append(raw)
        plane_raw = {}

        def load_plane(t):
            for c in range(T // PLANE_CHUNK):
                raw = keep.tile([P, PLANE_CHUNK], F32, name=f"plane_raw{t}_{c}")
                nc.sync.dma_start(raw[:], x_rows[:, t, c * PLANE_CHUNK : (c + 1) * PLANE_CHUNK])
                plane_raw[t, c] = raw

        w_raw = {}

        def load_weights(e):
            raw = keep.tile([P, PACK, N], F32, name=f"w_raw{e}")
            nc.sync.dma_start(raw[:], w[e].rearrange("(p j) n -> p j n", j=PACK))
            w_raw[e, 0] = raw

        load_plane(2)
        bias = keep.tile([P, BLOCKS, E], F32, name="bias")
        first_gates = keep.tile([P, C], F32, name="first_gates")
        rest_gates = keep.tile([P, T - C], F32, name="rest_gates")
        load_plane(3)
        rows = w[0].rearrange("(p j) n -> p j n", j=PACK)
        for h in range(2):
            raw = keep.tile([P, PACK, HALF], F32, name=f"w_raw0_{h}")
            nc.sync.dma_start(raw[:], rows[:, :, h * HALF : (h + 1) * HALF])
            w_raw[0, h] = raw
            if h == 0:
                nc.sync.dma_start(first_gates[:], gate[0:P, 0:C])
        nc.sync.dma_start(bias[:], b.rearrange("(n p) e -> p n e", p=P))
        load_weights(1)
        nc.sync.dma_start(rest_gates[:], gate[0:P, C:T])
        for e in range(2, E):
            load_weights(e)

        def gate_of(experts):
            lo, hi = experts[0] * C, (experts[-1] + 1) * C
            return first_gates[:] if lo == 0 else rest_gates[:, lo - C : hi - C]

        def list_of(experts):
            return offsets[:, experts[0] * C // 16 : (experts[-1] + 1) * C // 16]

        warm = keep.tile([P, 1], F32, name="warm")
        nc.vector.memset(warm[:], 0.0)
        nc.scalar.activation(warm[:], warm[:], RELU)

        def interleave(copy, dst, src):
            copy(
                dst.rearrange("p (c i) j -> p c j i", i=RUN),
                src.rearrange("p j (c i) -> p c j i", i=RUN),
            )

        pair = keep.tile([P, T, 2], BF16, name="pair")
        for (lo, hi), raw in zip(PAIR_CHUNKS, pair_raw):
            copy = nc.scalar.copy if lo == 0 else nc.vector.tensor_copy
            interleave(copy, pair[:, lo:hi, :], raw[:])
        words = pair[:].rearrange("p t j -> p (t j)").bitcast(U32)
        planes = keep.tile([P, PACK, T], BF16, name="planes", align_bytes=64)

        grouped = {}
        x_codes = [keep.tile([P, C], U32, name=f"x_codes{e}", align_bytes=64) for e in range(E)]
        x_scales = [keep.tile([P, C], U8, name=f"x_scales{e}", align_bytes=64) for e in range(E)]
        w_codes = [keep.tile([P, N], U32, name=f"w_codes{e}", align_bytes=64) for e in range(E)]
        w_scales = [keep.tile([P, N], U8, name=f"w_scales{e}", align_bytes=64) for e in range(E)]
        results = [keep.tile([P, T], F32, name=f"result{n}") for n in range(BLOCKS)]

        def round_plane(t, c, copy):
            copy(planes[:, t, c * PLANE_CHUNK : (c + 1) * PLANE_CHUNK], plane_raw[t, c][:])

        def gather(e):
            grouped[e] = ring.tile([P, C, PACK], BF16, name="grouped", align_bytes=64)
            if e < BY_PAIRS:
                gather_pair(e)
            for t in range(2 if e < BY_PAIRS else 0, PACK):
                gather_plane(e, t)
            quantise_tokens(e)

        def gather_pair(e):
            dst = grouped[e][:].rearrange("p s j -> p (s j)").bitcast(U32).rearrange("p (s u) -> p s u", u=2)
            nc.vector.tensor_copy(dst[:, :, 0], words.indirect(list_of([e])))

        def gather_plane(e, t):
            nc.scalar.activation(grouped[e][:, :, t], planes[:, t, :].indirect(list_of([e])), COPY)

        def quantise_tokens(e):
            nc.vector.quantize_mx(
                out=x_codes[e][:].bitcast(FP8X4),
                scales=x_scales[e][:],
                in_=grouped[e][:].rearrange("p s j -> p (s j)"),
            )

        def quantise_weights(e, h, copy):
            raw = w_raw[e, h]
            width = raw.shape[2]
            w_grouped = stage.tile([P, width, PACK], BF16, name="w_grouped", align_bytes=64)
            interleave(copy, w_grouped[:], raw[:])
            cols = slice(h * width, (h + 1) * width)
            nc.vector.quantize_mx(
                out=w_codes[e][:, cols].bitcast(FP8X4),
                scales=w_scales[e][:, cols],
                in_=w_grouped[:].rearrange("p n j -> p (n j)"),
            )

        group_of = {e: experts for experts in SCATTERS for e in experts}
        ys = {}

        def multiply(e, n):
            experts = group_of[e]
            cols = slice(n * P, (n + 1) * P)
            acc = psum.tile([P, C], F32, name="acc")
            nc.tensor.matmul_mx(
                out=acc[:],
                lhsT=w_codes[e][:, cols].bitcast(FP8X4),
                lhsT_scale=w_scales[e][:, cols],
                rhs=x_codes[e][:].bitcast(FP8X4),
                rhs_scale=x_scales[e][:],
                start=True,
                stop=True,
            )
            if e == experts[0]:
                y = work.tile([P, len(experts) * C], F32, name="y")
                ys[e, n] = y
            lo = (e - experts[0]) * C
            nc.scalar.activation(ys[experts[0], n][:, lo : lo + C], acc[:], RELU, bias=bias[:, n, e : e + 1])

        def put_back(experts):
            for n in range(BLOCKS):
                y = ys[experts[0], n]
                nc.vector.tensor_tensor(results[n][:].indirect(list_of(experts)), y[:], gate_of(experts), MULT)

        grouped[0] = ring.tile([P, C, PACK], BF16, name="grouped", align_bytes=64)
        gather_pair(0)
        for (lo, hi), raw in zip(PAIR_CHUNKS, pair_raw):
            nc.vector.tensor_copy(planes[:, 0:2, lo:hi], raw[:])
        round_plane(2, 0, nc.scalar.copy)
        round_plane(2, 1, nc.vector.tensor_copy)
        gather_plane(0, 2)
        round_plane(3, 0, nc.vector.tensor_copy)
        round_plane(3, 1, nc.vector.tensor_copy)
        gather_plane(0, 3)
        quantise_tokens(0)
        for h in range(2):
            quantise_weights(0, h, (nc.vector.tensor_copy, nc.scalar.copy)[h])
            for n in (2 * h, 2 * h + 1):
                multiply(0, n)
        gathered, quantised = 0, 0
        for e in range(E):
            while gathered < min(E - 1, e + GATHER_AHEAD[e]):
                gathered += 1
                gather(gathered)
            while quantised < min(E - 1, e + WEIGHTS_AHEAD[e]):
                quantised += 1
                quantise_weights(quantised, 0, nc.scalar.copy)
            if e > 0:
                for n in range(BLOCKS):
                    multiply(e, n)
            if e == group_of[e][-1]:
                put_back(group_of[e])

        for n in range(BLOCKS):
            nc.sync.dma_start(out[n * P : (n + 1) * P, :], results[n][:])
